import numpy as np
import ml_dtypes


def mxq(x, axis, fmt="e4m3"):
    dtype, down = {"e4m3": (ml_dtypes.float8_e4m3fn, 7), "e5m2": (ml_dtypes.float8_e5m2, 14)}[fmt]
    v = np.moveaxis(np.asarray(x, np.float32).astype(ml_dtypes.bfloat16).astype(np.float64), axis, -1)
    blocks = v.reshape(v.shape[:-1] + (-1, 32))
    amax = np.abs(blocks).max(-1, keepdims=True)
    byte = np.maximum(np.where(amax > 0, np.frexp(amax)[1] - 1 + 127, 0) - down, 1)
    scale = np.exp2(byte - 127.0)
    codes = (blocks / scale).astype(np.float32).astype(dtype).astype(np.float64)
    return np.moveaxis((codes * scale).reshape(v.shape), -1, axis)


WIDE = False


def mx_kscale(k):
    if not WIDE:
        return np.ones(k)
    levels = np.array([10, -10, 5, -5, 0])
    if k % 512:
        return np.exp2(np.random.permutation(np.resize(levels, k // 32))).repeat(32)
    a = np.empty((k // 512, 16))
    for p in range(k // 512):
        a[p, :8] = np.random.permutation(np.resize(levels, 8))
        for g in range(8):
            far = levels[np.abs(levels - a[p, g]) >= 10]
            a[p, g + 8] = far[np.random.randint(len(far))]
    return np.exp2(a.ravel()).repeat(32)


BF16 = ml_dtypes.bfloat16


def bf(x):
    return np.asarray(x, np.float32).astype(BF16)


def f64(x):
    return np.asarray(x).astype(np.float64)


E2M1 = np.array([0.0, 0.5, 1.0, 1.5, 2.0, 3.0, 4.0, 6.0, -0.0, -0.5, -1.0, -1.5, -2.0, -3.0, -4.0, -6.0])


def pack_weight(w, fmt):
    k, n = w.shape
    w = f64(bf(w)).reshape(k // 32, 32, n)
    amax = np.abs(w).max(1)
    if fmt == "e4m3":
        byte = np.frexp(amax)[1] - 1 + 127 - 7
    else:
        mant, ex = np.frexp(amax / 6.0)
        byte = np.where(mant > 0.5, ex, ex - 1) + 127
    byte = np.clip(np.where(amax > 0, byte, 1), 1, 254)
    scaled = (w * np.exp2(127.0 - byte)[:, None, :]).reshape(k, n).astype(np.float32)
    by_word = np.ascontiguousarray(scaled.reshape(k // 512, 128, 4, n).transpose(0, 1, 3, 2))
    if fmt == "e4m3":
        words = by_word.astype(ml_dtypes.float8_e4m3fn).view(np.uint8)
    else:
        c = by_word.astype(ml_dtypes.float4_e2m1fn).view(np.uint8) & 0xF
        words = c[..., 0::2] | (c[..., 1::2] << 4)
    return np.ascontiguousarray(words), np.ascontiguousarray(byte.astype(np.uint8).reshape(k // 512, 16, n))


def unpack_weight(words, scales, fmt):
    g, p, n, _ = words.shape
    if fmt == "e4m3":
        vals = np.ascontiguousarray(words).view(ml_dtypes.float8_e4m3fn).astype(np.float64)
    else:
        nib = np.empty((g, p, n, 4), np.uint8)
        nib[..., 0::2] = words & 0xF
        nib[..., 1::2] = words >> 4
        vals = E2M1[nib]
    vals = vals * np.repeat(np.exp2(scales.astype(np.float64) - 127.0), 8, axis=1)[..., None]
    return vals.transpose(0, 1, 3, 2).reshape(g * 512, n)
def pack4(w):
    words, scales = pack_weight(w, "e2m1")
    return words.reshape(words.shape[0], 128, -1), scales


def unpack4(words, scales):
    return unpack_weight(words.reshape(words.shape[0], 128, -1, 2), scales, "e2m1")


def planes(Y):
    n, m = Y.shape
    b = f64(bf(Y)).reshape(n // 32, 32, m)
    amax = np.abs(b).max(1)
    byte = np.clip(np.where(amax > 0, np.frexp(amax)[1] - 1 + 127 - 7, 1), 1, 254)
    codes = (b * np.exp2(127.0 - byte)[:, None, :]).reshape(n, m).astype(np.float32).astype(ml_dtypes.float8_e4m3fn).view(np.uint8)
    words = codes.reshape(n // 512, 128, 4, m).transpose(0, 1, 3, 2)
    return np.ascontiguousarray(words), np.ascontiguousarray(byte.astype(np.uint8).reshape(n // 512, 16, m))


T, C, L, P, F = 4, 8, 64, 1024, 1024

def fourier_matrix():
    freq = np.arange(F // 2) + 0.25 + 0.5 * np.random.rand(F // 2)
    angle = 2.0 * np.pi * np.arange(P)[:, None] * freq[None, :] / P
    return np.sqrt(2.0 / P) * np.concatenate([np.cos(angle), np.sin(angle)], axis=1)

def setup_inputs():
    s = mx_kscale(P)
    t = mx_kscale(F)
    X = 2.0 * np.random.randn(T * C * L, P)
    E = fourier_matrix()
    x_words, x_scales = pack_weight(X.T * s[:, None], "e4m3")
    fwd_words, fwd_scales = pack4(E / s[:, None] * t[None, :])
    mask = bf(1.0 / (1.0 + np.exp(-2.0 * np.random.randn(T, F))))
    adj = bf(E.T / t[:, None])
    lam = bf(0.05 + 0.1 * np.abs(np.random.randn(P)))
    profile = np.exp(0.8 * np.random.randn(P))
    coil = bf(profile * (1.0 + 0.3 * np.random.randn(C, L, P)))
    return {"x_words": x_words, "x_scales": x_scales, "fwd_words": fwd_words, "fwd_scales": fwd_scales,
            "mask": mask, "adj": adj, "lam": lam, "coil": coil}

def reference(x_words, x_scales, fwd_words, fwd_scales, mask, adj, lam, coil):
    xt = unpack_weight(x_words, x_scales, "e4m3")
    e = unpack4(fwd_words, fwd_scales)
    mask, lam, coil = f64(mask), f64(lam), f64(coil)
    spec = xt.T @ e
    h = (spec.reshape(T, C * L, F) * mask[:, None, :]).reshape(T * C * L, F)
    z = (mxq(h, 1, "e4m3") @ mxq(f64(adj), 0, "e4m3")).reshape(T, C, L, P)
    y = (z - np.minimum(np.maximum(z, -lam), lam)) * coil
    Y = y.reshape(T * C * L, P).T
    words, scales = planes(Y)
    return y, words, scales

@@ -1,0 +1,376 @@
+from contextlib import ExitStack
+
+import concourse.mybir as mybir
+from concourse.masks import make_identity
+
+F32 = mybir.dt.float32
+BF16 = mybir.dt.bfloat16
+I32 = mybir.dt.int32
+U32 = mybir.dt.uint32
+U8 = mybir.dt.uint8
+FP8X4 = mybir.dt.float8_e4m3fn_x4
+FP4X4 = mybir.dt.float4_e2m1fn_x4
+ALU = mybir.AluOpType
+ACT = mybir.ActivationFunctionType
+
+P = 128
+FRAMES = 4
+ROWS = 512
+GROUPS = 2
+FLOPS = 2 * 2 * 2048 * 1024 * 1024
+
+HEAD = [('adj_weave', 0, 0, 0, 2, 'scalar'), ('adj_weave', 0, 0, 2, 4, 'vector'), 's', 's', 's', 's', ('adj_weave', 1, 0, 0, 4, 'vector'), ('adj_quant', 0, 0), ('h_weave', 0, 0, 0, 512, 'vector'), ('adj_quant', 1, 0), 's', 's', 's', 's', ('h_quant', 0, 0), ('h_weave', 0, 1, 0, 192, 'scalar'), ('h_weave', 0, 1, 192, 512, 'vector'), ('h_quant', 0, 1), 's', 's', 's', 's', 's', ('adj_weave', 0, 1, 0, 4, 'vector'), ('adj_weave', 1, 1, 0, 4, 'vector')]
+EARLY = {0: [('h_weave', 1, 0, 0, 512, 'gpsimd')]}
+SIDE = {0: ['s', 's', 's', ('h_weave', 1, 1, 0, 256, 'scalar'), 's', 's'], 1: ['s', 's', ('h_weave', 2, 0, 0, 256, 'scalar'), 's', 's', 's'], 2: ['s', ('h_weave', 2, 1, 0, 256, 'scalar'), 's'], 3: ['s', 's', 's', ('h_weave', 3, 0, 0, 256, 'scalar')], 4: ['s', 's', 's', 's', ('h_weave', 3, 1, 0, 256, 'scalar')], 5: [('h_weave', 3, 1, 256, 512, 'scalar')]}
+WINDOW = {0: [('adj_quant', 0, 1), ('adj_quant', 1, 1), ('h_quant', 1, 0)], 1: [('h_weave', 1, 1, 256, 512, 'vector'), ('h_weave', 2, 0, 256, 512, 'vector'), ('h_quant', 1, 1)], 2: [('h_weave', 2, 1, 256, 512, 'vector'), ('h_quant', 2, 0)], 3: [('h_weave', 3, 0, 256, 512, 'vector'), ('h_quant', 2, 1)], 4: [('h_quant', 3, 0)], 5: [('h_quant', 3, 1)]}
+CAST = {(8, 1): "scalar", (8, 2): "gpsimd", (8, 3): "scalar"}
+TAIL = ((0, 2), (2, 3), (3, 4))
+
+
+def schedule():
+    units = [(fr, g) for fr in range(FRAMES) for g in range(GROUPS)]
+    count = len(units)
+    todo = [(fr, gf, t) for fr in range(FRAMES) for gf in range(GROUPS) for t in range(4)]
+    taken = []
+    held = []
+
+    def bank():
+        taken.append(len(taken) % 8)
+        return taken[-1]
+
+    def side(items):
+        out = []
+        for e in items:
+            if e == "s" or e == "v":
+                b = todo.pop(0)
+                out += [("spec_mm",) + b + (bank(),)]
+                if e == "s":
+                    out += [("spec_out",) + b + ("scalar",)]
+                else:
+                    held.append(("spec_out",) + b + ("vector",))
+            else:
+                out += [e]
+        return out
+
+    ops = [("setup",), ("e_scale_perm",), ("mask_perm",), ("mask_turn", bank()), ("e_perm",), ("mask_out",), ("lam",)]
+    ops += side(HEAD)
+    for k in range(count + 1):
+        if k >= 1:
+            for rb in range(4):
+                ops += [("y_out", units[k - 1], rb, (k - 1) % 3)]
+                ops += [("cast", units[k - 1], rb, rb + 1, (k - 1) % 3, (k - 1) % 2, CAST.get((k, rb), "gpsimd"))]
+                if k == count:
+                    ops += [("y_store", units[k - 1], rb, rb + 1, (k - 1) % 3)]
+                elif rb % 2 == 1:
+                    ops += [("y_store", units[k - 1], rb - 1, rb + 1, (k - 1) % 3)]
+        ops += EARLY.get(k, []) + held
+        held.clear()
+        if k < count:
+            ops += [("pix_mm", units[k], t, bank()) for t in range(4)] + [("relu", units[k], t) for t in range(4)]
+            ops += [("soft", units[k], t, k % 2) for t in range(4)]
+        ops += side(SIDE.get(k, []))
+        if k >= 1:
+            for r0, r1 in ((0, 2), (2, 4)) if k < count else TAIL:
+                ops += [("word_turn", units[k - 1], r0, r1, (k - 1) % 2, bank()), ("word_out", units[k - 1], r0, r1, (k - 1) % 2, "scalar")]
+        if k < count:
+            ops += [("turn", units[k], rb, k % 2, bank()) for rb in range(4)]
+        ops += WINDOW.get(k, [])
+        if k >= 2:
+            ops += [("plane_quant", units[k - 2], 0, 512, k % 2, (k - 2) % 3), ("word_store", units[k - 2], 0, 512, (k - 2) % 3)]
+        if k == 7:
+            ops += [("scale_store", 0, 3 * ROWS)]
+    end = units[-1]
+    for r0, r1 in TAIL:
+        ops += [("plane_quant", end, P * r0, P * r1, 1, 1), ("word_store", end, P * r0, P * r1, 1)]
+    ops += [("scale_store", 3 * ROWS, 4 * ROWS)]
+    return ops
+
+
+def tile_masked_fourier_soft_threshold_h2_kernel(
+    tc, x_words, x_scales, fwd_words, fwd_scales, mask, adj, lam, coil, out_0, out_1, out_2
+):
+    nc = tc.nc
+    with ExitStack() as ctx:
+        sb = ctx.enter_context(tc.tile_pool(name="sb", bufs=1))
+        ps = ctx.enter_context(tc.psum_pool(name="ps", bufs=1))
+        ctx.enter_context(tc.manual_schedule())
+
+        def tiles(name, count, shape, dtype):
+            return [sb.tile(shape, dtype, name="%s%d" % (name, i), align_bytes=64) for i in range(count)]
+
+        banks = [ps.tile([P, 512], F32, name="bank%d" % i) for i in range(8)]
+        e_raw = sb.tile([P, GROUPS, 2048], U8, align_bytes=64)
+        e_words = sb.tile([P, GROUPS, 2048], U8, align_bytes=64)
+        e_scale_raw = sb.tile([P, GROUPS, 1024], U8, align_bytes=64)
+        e_scale = sb.tile([P, GROUPS, 1024], U8, align_bytes=64)
+        x_codes = tiles("x_codes", FRAMES, [P, GROUPS, ROWS], U32)
+        x_scale = sb.tile([P, GROUPS, FRAMES * ROWS], U8, align_bytes=64)
+        adj_raw = tiles("adj_raw", 4, [P, 4, 512], BF16)
+        adj_woven = tiles("adj_woven", 4, [P, 2048], BF16)
+        adj_codes = tiles("adj_codes", 4, [P, 512], U32)
+        adj_scale = tiles("adj_scale", 4, [P, 512], U8)
+        coil_rows = sb.tile([P, 4, 1024], BF16, align_bytes=64)
+        ident = sb.tile([P, P], F32, align_bytes=64)
+        mask_raw = sb.tile([8, 512], BF16, align_bytes=64)
+        mask_rows = sb.tile([P, 512], F32, align_bytes=64)
+        mask_cols = sb.tile([P, 4, 8], F32, align_bytes=64)
+        lam_raw = sb.tile([P, GROUPS, 4], BF16, align_bytes=64)
+        lam_abs = sb.tile([P, GROUPS, 4], F32, align_bytes=64)
+        lam_lift = sb.tile([P, GROUPS, 4], F32, align_bytes=64)
+        lam_bias = sb.tile([P, GROUPS, 4], F32, align_bytes=64)
+        warm = sb.tile([P, 1], F32, align_bytes=64)
+        h_raw = tiles("h_raw", 4, [P, 4, ROWS], BF16)
+        h_woven = tiles("h_woven", 2, [P, ROWS, 4], BF16) + [adj_raw[3][:].rearrange("p j (a t) -> p (j a) t", t=4)]
+        h_codes = tiles("h_codes", 8, [P, ROWS], U32)
+        h_scale = tiles("h_scale", 8, [P, ROWS], U8)
+        above = tiles("above", 4, [P, ROWS], F32)
+        soft = tiles("soft", 2, [P, 4, ROWS], F32)
+        y_rows = tiles("y_rows", 3, [P, 4, 512], F32)
+        y_pairs = tiles("y_pairs", 2, [P, 4, 512], BF16)
+        y_woven = tiles("y_woven", 2, [P, ROWS, 4], BF16)
+        y_codes = tiles("y_codes", 3, [P, ROWS], U32)
+        y_scale = sb.tile([P, GROUPS, FRAMES * ROWS], U8, align_bytes=64)
+
+        x_hbm = x_words.rearrange("g p n t -> p g (n t)")
+        y_hbm = out_0.rearrange("i c l n -> i (c l) n")
+        words_hbm = out_1.rearrange("g p m t -> g p (m t)")
+        bank_of = {}
+
+        def take_bank(key, index):
+            bank_of[key] = banks[index]
+            return bank_of[key]
+
+        def move(engine, dst, src):
+            if engine == "gpsimd":
+                nc.gpsimd.tensor_scalar(out=dst, in0=src, scalar1=1.0, scalar2=1.0, op0=ALU.mult, op1=ALU.mult)
+            elif engine == "vector":
+                nc.vector.tensor_copy(out=dst, in_=src)
+            else:
+                nc.scalar.copy(out=dst, in_=src)
+
+        def load_scale_rows(plane, rows, q):
+            nc.sync.dma_start(
+                out=plane[32 * q : 32 * q + 4, :, :].bitcast(I32),
+                in_=rows[:, 4 * q : 4 * q + 4, :].rearrange("g r n -> r g n").bitcast(I32),
+            )
+
+        def load_x(fr):
+            nc.sync.dma_start(out=x_codes[fr][:].bitcast(I32), in_=x_hbm[:, :, 2048 * fr : 2048 * (fr + 1)].bitcast(I32))
+
+        def load_adj(g):
+            for gf in range(GROUPS):
+                src = adj[512 * gf : 512 * (gf + 1), 512 * g : 512 * (g + 1)].rearrange("(q t b) n -> b q t n", t=4, b=4)
+                for b in range(4):
+                    nc.sync.dma_start(out=adj_raw[2 * gf + g][b:P:4, :, :], in_=src[b])
+
+        def load_coil():
+            nc.sync.dma_start(out=coil_rows[:], in_=coil.rearrange("c l n -> (c l) n").rearrange("(b r) n -> r b n", r=P))
+
+        def setup():
+            nc.vector.memset(e_scale_raw[:].bitcast(I32), 0)
+            nc.vector.memset(x_scale[:].bitcast(I32), 0)
+            nc.vector.memset(mask_rows[:], 0.0)
+            nc.vector.memset(warm[:], 0.0)
+            nc.scalar.activation(out=warm[:], in_=warm[:], func=ACT.Relu)
+            nc.gpsimd.dma_start(out=mask_raw[:], in_=mask.rearrange("i (g f) -> (i g) f", g=GROUPS))
+            nc.gpsimd.dma_start(out=lam_raw[:], in_=lam.rearrange("(g p t) -> p g t", g=GROUPS, t=4))
+            make_identity(nc, ident[:])
+            for q in range(4):
+                load_scale_rows(e_scale_raw, fwd_scales, q)
+            for q in range(2):
+                load_scale_rows(x_scale, x_scales, q)
+            nc.sync.dma_start(out=e_raw[:].bitcast(I32), in_=fwd_words.rearrange("g p b -> p g b").bitcast(I32))
+            load_x(0)
+            for q in range(2, 4):
+                load_scale_rows(x_scale, x_scales, q)
+            load_adj(0)
+            load_x(1)
+            load_adj(1)
+            load_coil()
+            load_x(2)
+            load_x(3)
+
+        def e_scale_perm():
+            nc.vector.tensor_copy(
+                out=e_scale[:].bitcast(I32).rearrange("p g (h t q) -> p (g h) t q", h=2, t=4),
+                in_=e_scale_raw[:].bitcast(I32).rearrange("p g (h q t) -> p (g h) t q", h=2, t=4),
+            )
+
+        def e_perm():
+            for gf in range(GROUPS):
+                for g in range(GROUPS):
+                    cols = slice(256 * gf, 256 * (gf + 1))
+                    nc.vector.tensor_copy(
+                        out=e_words[:].bitcast(I32)[:, g, cols].rearrange("p (t q b) -> p t q b", t=4, b=2),
+                        in_=e_raw[:].bitcast(I32)[:, g, cols].rearrange("p (q t b) -> p t q b", t=4, b=2),
+                    )
+
+        def mask_perm():
+            nc.vector.tensor_copy(
+                out=mask_rows[0:8, :].rearrange("p (t q b) -> p t q b", t=4, b=4),
+                in_=mask_raw[:].rearrange("p (q t b) -> p t q b", t=4, b=4),
+            )
+
+        def mask_turn(index):
+            bank = take_bank("mask", index)
+            for t in range(4):
+                nc.tensor.transpose(bank[:, P * t : P * (t + 1)], mask_rows[:, P * t : P * (t + 1)], ident[:])
+
+        def mask_out():
+            nc.vector.tensor_copy(out=mask_cols[:], in_=bank_of["mask"][:].rearrange("p (t r) -> p t r", t=4)[:, :, 0:8])
+
+        def lam_prepare():
+            nc.vector.scalar_tensor_tensor(
+                out=lam_abs[:], in0=lam_raw[:], scalar=-1.0, in1=lam_raw[:], op0=ALU.mult, op1=ALU.max
+            )
+            nc.gpsimd.tensor_scalar(
+                out=lam_lift[:], in0=lam_raw[:], scalar1=0.0, scalar2=2.0**126, op0=ALU.is_lt, op1=ALU.mult
+            )
+            nc.gpsimd.tensor_tensor(out=lam_bias[:], in0=lam_lift[:], in1=lam_raw[:], op=ALU.subtract)
+
+        def spec_mm(fr, gf, t, index):
+            bank = take_bank(("spec", fr, gf, t), index)
+            col = 512 * gf + P * t
+            for g in range(GROUPS):
+                nc.tensor.matmul_mx(
+                    out=bank[:],
+                    lhsT=e_words[:, g, 2 * col : 2 * (col + P)].bitcast(FP4X4),
+                    lhsT_scale=e_scale[:, g, col : col + P],
+                    rhs=x_codes[fr][:, g, :].bitcast(FP8X4),
+                    rhs_scale=x_scale[:, g, ROWS * fr : ROWS * (fr + 1)],
+                    start=(g == 0),
+                    stop=(g == GROUPS - 1),
+                )
+
+        def spec_out(fr, gf, t, engine):
+            k = 2 * fr + gf
+            bank = bank_of[("spec", fr, gf, t)]
+            factor = mask_cols[:, t, k : k + 1]
+            if engine == "vector":
+                nc.vector.tensor_scalar(out=h_raw[k % 4][:, t, :], in0=bank[:], scalar1=factor, scalar2=None, op0=ALU.mult)
+            else:
+                nc.scalar.activation(out=h_raw[k % 4][:, t, :], in_=bank[:], func=ACT.Copy, scale=factor)
+
+        def h_weave(fr, gf, c0, c1, engine):
+            k = 2 * fr + gf
+            dst = h_woven[k % 3][:, c0:c1, :].rearrange("p (c i) t -> p c t i", i=4)
+            src = h_raw[k % 4][:, :, c0:c1].rearrange("p t (c i) -> p c t i", i=4)
+            move(engine, dst, src)
+
+        def h_quant(fr, gf):
+            k = 2 * fr + gf
+            nc.vector.quantize_mx(
+                out=h_codes[k][:].bitcast(FP8X4), scales=h_scale[k][:],
+                in_=h_woven[k % 3][:].rearrange("p r t -> p (r t)"),
+            )
+
+        def adj_weave(gf, g, t0, t1, engine):
+            dst = adj_woven[2 * gf + g][:].rearrange("p (t m j) -> p t m j", t=4, j=4)[:, t0:t1]
+            src = adj_raw[2 * gf + g][:].rearrange("p j (m t) -> p t m j", t=4)[:, t0:t1]
+            move(engine, dst, src)
+
+        def adj_quant(gf, g):
+            k = 2 * gf + g
+            nc.vector.quantize_mx(out=adj_codes[k][:].bitcast(FP8X4), scales=adj_scale[k][:], in_=adj_woven[k][:])
+
+        def pix_mm(unit, t, index):
+            fr, g = unit
+            bank = take_bank(("pix", unit, t), index)
+            for gf in range(GROUPS):
+                nc.tensor.matmul_mx(
+                    out=bank[:],
+                    lhsT=adj_codes[2 * gf + g][:, P * t : P * (t + 1)].bitcast(FP8X4),
+                    lhsT_scale=adj_scale[2 * gf + g][:, P * t : P * (t + 1)],
+                    rhs=h_codes[2 * fr + gf][:].bitcast(FP8X4),
+                    rhs_scale=h_scale[2 * fr + gf][:],
+                    start=(gf == 0),
+                    stop=(gf == GROUPS - 1),
+                )
+
+        def relu(unit, t):
+            fr, g = unit
+            nc.scalar.activation(
+                out=above[t][:], in_=bank_of[("pix", unit, t)][:], func=ACT.Relu, bias=lam_bias[:, g, t : t + 1]
+            )
+
+        def soft_min(unit, t, slot):
+            fr, g = unit
+            nc.vector.scalar_tensor_tensor(
+                out=soft[slot][:, t, :], in0=bank_of[("pix", unit, t)][:], scalar=lam_abs[:, g, t : t + 1],
+                in1=above[t][:], op0=ALU.add, op1=ALU.min,
+            )
+
+        def turn(unit, rb, slot, index):
+            bank = take_bank(("turn", unit, rb), index)
+            for t in range(4):
+                nc.tensor.transpose(bank[:, P * t : P * (t + 1)], soft[slot][:, t, P * rb : P * (rb + 1)], ident[:])
+
+        def y_out(unit, rb, slot):
+            fr, g = unit
+            nc.vector.tensor_tensor(
+                out=y_rows[slot][:, rb, :].rearrange("r (p t) -> r p t", t=4),
+                in0=bank_of[("turn", unit, rb)][:].rearrange("r (t p) -> r p t", t=4),
+                in1=coil_rows[:, rb, 512 * g : 512 * (g + 1)].rearrange("r (p t) -> r p t", t=4),
+                op=ALU.mult,
+            )
+
+        def y_store(unit, r0, r1, slot):
+            fr, g = unit
+            nc.sync.dma_start(
+                out=y_hbm[fr].rearrange("(b r) n -> r b n", r=P)[:, r0:r1, 512 * g : 512 * (g + 1)],
+                in_=y_rows[slot][:, r0:r1, :],
+            )
+
+        def cast(unit, r0, r1, slot, pslot, engine):
+            for rb in range(r0, r1):
+                dst = y_pairs[pslot][:, rb, :].rearrange("r (u p e) -> r u p e", u=2, e=2)
+                src = y_rows[slot][:, rb, :].rearrange("r (p u e) -> r u p e", u=2, e=2)
+                move(engine, dst, src)
+
+        def word_turn(unit, r0, r1, pslot, index):
+            bank = take_bank(("word", unit, r0), index)
+            words = y_pairs[pslot][:].bitcast(F32)
+            for j in range(r1 - r0):
+                for u in range(2):
+                    nc.tensor.transpose(
+                        bank[:, P * (2 * j + u) : P * (2 * j + u + 1)], words[:, r0 + j, P * u : P * (u + 1)], ident[:]
+                    )
+
+        def word_out(unit, r0, r1, pslot, engine):
+            dst = y_woven[pslot][:, P * r0 : P * r1, :].rearrange("p r t -> p (r t)").bitcast(F32)
+            src = bank_of[("word", unit, r0)][:, 0 : 2 * P * (r1 - r0)]
+            move(engine, dst.rearrange("p (j r u) -> p j r u", r=P, u=2), src.rearrange("p (j u r) -> p j r u", r=P, u=2))
+
+        def plane_quant(unit, c0, c1, pslot, slot):
+            fr, g = unit
+            nc.vector.quantize_mx(
+                out=y_codes[slot][:, c0:c1].bitcast(FP8X4),
+                scales=y_scale[:, g, ROWS * fr + c0 : ROWS * fr + c1],
+                in_=y_woven[pslot][:, c0:c1, :].rearrange("p r t -> p (r t)"),
+            )
+
+        def word_store(unit, c0, c1, slot):
+            fr, g = unit
+            nc.sync.dma_start(
+                out=words_hbm[g][:, 4 * (ROWS * fr + c0) : 4 * (ROWS * fr + c1)].bitcast(I32),
+                in_=y_codes[slot][:, c0:c1].bitcast(I32),
+            )
+
+        def scale_store(c0, c1):
+            for q in range(4):
+                queue = nc.scalar if (c1 == FRAMES * ROWS and q % 2 == 1) else nc.sync
+                queue.dma_start(
+                    out=out_2[:, 4 * q : 4 * q + 4, c0:c1].rearrange("g r n -> r g n").bitcast(I32),
+                    in_=y_scale[32 * q : 32 * q + 4, :, c0:c1].bitcast(I32),
+                )
+
+        steps = {
+            "setup": setup, "e_perm": e_perm, "e_scale_perm": e_scale_perm, "mask_perm": mask_perm,
+            "mask_turn": mask_turn, "mask_out": mask_out, "lam": lam_prepare, "spec_mm": spec_mm, "spec_out": spec_out,
+            "h_weave": h_weave, "h_quant": h_quant, "adj_weave": adj_weave, "adj_quant": adj_quant,
+            "cast": cast, "word_turn": word_turn, "word_out": word_out, "pix_mm": pix_mm, "relu": relu, "soft": soft_min,
+            "turn": turn, "y_out": y_out, "y_store": y_store, "plane_quant": plane_quant,
+            "word_store": word_store, "scale_store": scale_store,
+        }
+        for step in schedule():
+            steps[step[0]](*step[1:])

@@ -19,12 +19,18 @@ ROWS = 512
 GROUPS = 2
 FLOPS = 2 * 2 * 2048 * 1024 * 1024
 
-HEAD = [('adj_weave', 0, 0, 0, 2, 'scalar'), ('adj_weave', 0, 0, 2, 4, 'vector'), 's', 's', 's', 's', ('adj_weave', 1, 0, 0, 4, 'vector'), ('adj_quant', 0, 0), ('h_weave', 0, 0, 0, 512, 'vector'), ('adj_quant', 1, 0), 's', 's', 's', 's', ('h_quant', 0, 0), ('h_weave', 0, 1, 0, 192, 'scalar'), ('h_weave', 0, 1, 192, 512, 'vector'), ('h_quant', 0, 1), 's', 's', 's', 's', 's', ('adj_weave', 0, 1, 0, 4, 'vector'), ('adj_weave', 1, 1, 0, 4, 'vector')]
-EARLY = {0: [('h_weave', 1, 0, 0, 512, 'gpsimd')]}
-SIDE = {0: ['s', 's', 's', ('h_weave', 1, 1, 0, 256, 'scalar'), 's', 's'], 1: ['s', 's', ('h_weave', 2, 0, 0, 256, 'scalar'), 's', 's', 's'], 2: ['s', ('h_weave', 2, 1, 0, 256, 'scalar'), 's'], 3: ['s', 's', 's', ('h_weave', 3, 0, 0, 256, 'scalar')], 4: ['s', 's', 's', 's', ('h_weave', 3, 1, 0, 256, 'scalar')], 5: [('h_weave', 3, 1, 256, 512, 'scalar')]}
-WINDOW = {0: [('adj_quant', 0, 1), ('adj_quant', 1, 1), ('h_quant', 1, 0)], 1: [('h_weave', 1, 1, 256, 512, 'vector'), ('h_weave', 2, 0, 256, 512, 'vector'), ('h_quant', 1, 1)], 2: [('h_weave', 2, 1, 256, 512, 'vector'), ('h_quant', 2, 0)], 3: [('h_weave', 3, 0, 256, 512, 'vector'), ('h_quant', 2, 1)], 4: [('h_quant', 3, 0)], 5: [('h_quant', 3, 1)]}
-CAST = {(8, 1): "scalar", (8, 2): "gpsimd", (8, 3): "scalar"}
+HEAD = [('e_perm',), ('mask_perm',), 'm', ('e_scale_perm',), ('mask_out',), ('lam',), ('adj_weave', 0, 0, 0, 2, 'scalar'), ('adj_weave', 0, 0, 2, 4, 'vector'), 's', 's', 's', 's', ('adj_weave', 1, 0, 0, 4, 'vector'), ('adj_quant', 0, 0), ('h_weave', 0, 0, 0, 512, 'vector'), ('adj_quant', 1, 0), 's', 's', 's', 's', ('h_quant', 0, 0), ('h_weave', 0, 1, 0, 192, 'scalar'), ('h_weave', 0, 1, 192, 512, 'vector'), ('h_quant', 0, 1), 's', 's', 's', 's', 's', 's', ('adj_weave', 0, 1, 0, 4, 'vector'), ('adj_weave', 1, 1, 0, 4, 'vector')]
+EARLY = {0: [('h_weave', 1, 0, 128, 512, 'gpsimd')], 1: [('h_weave', 1, 1, 256, 384, 'gpsimd'), ('h_weave', 2, 0, 0, 128, 'gpsimd')], 2: [('h_weave', 2, 1, 0, 128, 'gpsimd'), ('h_weave', 2, 1, 384, 512, 'gpsimd')], 3: [('h_weave', 3, 0, 384, 512, 'gpsimd')]}
+SIDE = {0: ['s', 's', 's', 's', 's', 's'], 1: ['s', 's', 's', ('h_weave', 1, 1, 128, 256, 'scalar'), 's', 's', ('h_weave', 2, 0, 384, 512, 'scalar')], 2: ['s', 's', 's', ('h_weave', 2, 0, 128, 256, 'scalar'), ('h_weave', 2, 1, 128, 256, 'scalar')], 3: ['s', ('h_weave', 2, 1, 256, 384, 'scalar'), ('h_weave', 3, 0, 128, 256, 'scalar')], 4: ['s', 's', 's', ('h_weave', 3, 0, 256, 384, 'scalar'), ('h_weave', 3, 1, 128, 384, 'scalar')], 5: [('h_weave', 3, 1, 0, 128, 'scalar'), ('h_weave', 3, 1, 384, 512, 'scalar')]}
+WINDOW = {0: [('h_weave', 1, 0, 0, 128, 'vector'), ('adj_quant', 0, 1), ('adj_quant', 1, 1), ('h_quant', 1, 0)], 1: [('h_weave', 1, 1, 0, 128, 'vector'), ('h_weave', 1, 1, 384, 512, 'vector'), ('h_weave', 2, 0, 256, 384, 'vector'), ('h_quant', 1, 1)], 3: [('h_weave', 3, 0, 0, 128, 'vector'), ('h_quant', 2, 0), ('h_quant', 2, 1)], 5: [('h_quant', 3, 0), ('h_quant', 3, 1)]}
+AHEAD = {3: 1}
+WORDS_BEFORE = {1: [0], 3: [1, 2], 5: [3], 6: [4, 5], 7: [6]}
+WORDS_AFTER = {}
+PLANES = {2: [0], 4: [1, 2], 6: [3, 4], 7: [5], 8: [6]}
+LAST_CAST = ("gpsimd", "scalar", "gpsimd", "scalar")
 TAIL = ((0, 2), (2, 3), (3, 4))
+YS = 3
+CW = 1
 
 
 def schedule():
@@ -32,7 +38,6 @@ def schedule():
     count = len(units)
     todo = [(fr, gf, t) for fr in range(FRAMES) for gf in range(GROUPS) for t in range(4)]
     taken = []
-    held = []
 
     def bank():
         taken.append(len(taken) % 8)
@@ -41,48 +46,61 @@ def schedule():
     def side(items):
         out = []
         for e in items:
-            if e == "s" or e == "v":
+            if e == "s":
                 b = todo.pop(0)
-                out += [("spec_mm",) + b + (bank(),)]
-                if e == "s":
-                    out += [("spec_out",) + b + ("scalar",)]
-                else:
-                    held.append(("spec_out",) + b + ("vector",))
+                out += [("spec_mm",) + b + (bank(),), ("spec_out",) + b + ("scalar",)]
+            elif e == "m":
+                out += [("mask_turn", bank())]
             else:
                 out += [e]
         return out
 
-    ops = [("setup",), ("e_scale_perm",), ("mask_perm",), ("mask_turn", bank()), ("e_perm",), ("mask_out",), ("lam",)]
-    ops += side(HEAD)
+    def pix(k, ts):
+        if k >= count:
+            return []
+        return [("pix_mm", units[k], t, bank()) for t in ts] + [("relu", units[k], t) for t in ts] + [("soft", units[k], t, k % 2) for t in ts]
+
+    def words(u, cuts):
+        out = []
+        for r0, r1 in cuts:
+            out += [("word_turn", units[u], r0, r1, u % 2, bank()), ("word_out", units[u], r0, r1, u % 3, "scalar")]
+        return out
+
+    def planes(u, cuts):
+        out = []
+        for r0, r1 in cuts:
+            out += [("plane_quant", units[u], P * r0, P * r1, u % 3, u % 3), ("word_store", units[u], P * r0, P * r1, u % 3)]
+        return out
+
+    ops = [("setup",)] + side(HEAD)
     for k in range(count + 1):
         if k >= 1:
             for rb in range(4):
-                ops += [("y_out", units[k - 1], rb, (k - 1) % 3)]
-                ops += [("cast", units[k - 1], rb, rb + 1, (k - 1) % 3, (k - 1) % 2, CAST.get((k, rb), "gpsimd"))]
+                ops += [("y_out", units[k - 1], rb, (k - 1) % YS)]
                 if k == count:
-                    ops += [("y_store", units[k - 1], rb, rb + 1, (k - 1) % 3)]
-                elif rb % 2 == 1:
-                    ops += [("y_store", units[k - 1], rb - 1, rb + 1, (k - 1) % 3)]
-        ops += EARLY.get(k, []) + held
-        held.clear()
-        if k < count:
-            ops += [("pix_mm", units[k], t, bank()) for t in range(4)] + [("relu", units[k], t) for t in range(4)]
-            ops += [("soft", units[k], t, k % 2) for t in range(4)]
+                    ops += [("y_store", units[k - 1], rb, rb + 1, (k - 1) % YS)]
+                    ops += [("cast", units[k - 1], rb, rb + 1, (k - 1) % YS, (k - 1) % 2, LAST_CAST[rb])]
+                elif (rb + 1) % CW == 0:
+                    ops += [("cast", units[k - 1], rb + 1 - CW, rb + 1, (k - 1) % YS, (k - 1) % 2, "gpsimd")]
+                if k < count and rb % 2 == 1:
+                    ops += [("y_store", units[k - 1], rb - 1, rb + 1, (k - 1) % YS)]
+        ops += EARLY.get(k, [])
+        ops += pix(k, range(AHEAD.get(k, 0), 4)) + pix(k + 1, range(AHEAD.get(k + 1, 0)))
         ops += side(SIDE.get(k, []))
-        if k >= 1:
-            for r0, r1 in ((0, 2), (2, 4)) if k < count else TAIL:
-                ops += [("word_turn", units[k - 1], r0, r1, (k - 1) % 2, bank()), ("word_out", units[k - 1], r0, r1, (k - 1) % 2, "scalar")]
+        for u in WORDS_BEFORE.get(k, []):
+            ops += words(u, ((0, 2), (2, 4)))
         if k < count:
             ops += [("turn", units[k], rb, k % 2, bank()) for rb in range(4)]
+        for u in WORDS_AFTER.get(k, []):
+            ops += words(u, ((0, 2), (2, 4)))
+        if k == count:
+            ops += words(count - 1, TAIL)
         ops += WINDOW.get(k, [])
-        if k >= 2:
-            ops += [("plane_quant", units[k - 2], 0, 512, k % 2, (k - 2) % 3), ("word_store", units[k - 2], 0, 512, (k - 2) % 3)]
-        if k == 7:
-            ops += [("scale_store", 0, 3 * ROWS)]
-    end = units[-1]
-    for r0, r1 in TAIL:
-        ops += [("plane_quant", end, P * r0, P * r1, 1, 1), ("word_store", end, P * r0, P * r1, 1)]
-    ops += [("scale_store", 3 * ROWS, 4 * ROWS)]
+        for u in PLANES.get(k, []):
+            ops += planes(u, ((0, 4),))
+            if u == 5:
+                ops += [("scale_store", 0, 3 * ROWS)]
+    ops += planes(count - 1, TAIL) + [("scale_store", 3 * ROWS, 4 * ROWS)]
     return ops
 
 
@@ -104,7 +122,8 @@ def tile_masked_fourier_soft_threshold_h2_kernel(
         e_scale_raw = sb.tile([P, GROUPS, 1024], U8, align_bytes=64)
         e_scale = sb.tile([P, GROUPS, 1024], U8, align_bytes=64)
         x_codes = tiles("x_codes", FRAMES, [P, GROUPS, ROWS], U32)
-        x_scale = sb.tile([P, GROUPS, FRAMES * ROWS], U8, align_bytes=64)
+        x_scale_first = sb.tile([P, GROUPS, ROWS], U8, align_bytes=64)
+        x_scale_rest = sb.tile([P, GROUPS, (FRAMES - 1) * ROWS], U8, align_bytes=64)
         adj_raw = tiles("adj_raw", 4, [P, 4, 512], BF16)
         adj_woven = tiles("adj_woven", 4, [P, 2048], BF16)
         adj_codes = tiles("adj_codes", 4, [P, 512], U32)
@@ -127,7 +146,7 @@ def tile_masked_fourier_soft_threshold_h2_kernel(
         soft = tiles("soft", 2, [P, 4, ROWS], F32)
         y_rows = tiles("y_rows", 3, [P, 4, 512], F32)
         y_pairs = tiles("y_pairs", 2, [P, 4, 512], BF16)
-        y_woven = tiles("y_woven", 2, [P, ROWS, 4], BF16)
+        y_woven = tiles("y_woven", 3, [P, ROWS, 4], BF16)
         y_codes = tiles("y_codes", 3, [P, ROWS], U32)
         y_scale = sb.tile([P, GROUPS, FRAMES * ROWS], U8, align_bytes=64)
 
@@ -168,23 +187,24 @@ def tile_masked_fourier_soft_threshold_h2_kernel(
 
         def setup():
             nc.vector.memset(e_scale_raw[:].bitcast(I32), 0)
-            nc.vector.memset(x_scale[:].bitcast(I32), 0)
+            nc.vector.memset(x_scale_first[:].bitcast(I32), 0)
             nc.vector.memset(mask_rows[:], 0.0)
+            nc.vector.memset(x_scale_rest[:].bitcast(I32), 0)
             nc.vector.memset(warm[:], 0.0)
             nc.scalar.activation(out=warm[:], in_=warm[:], func=ACT.Relu)
             nc.gpsimd.dma_start(out=mask_raw[:], in_=mask.rearrange("i (g f) -> (i g) f", g=GROUPS))
             nc.gpsimd.dma_start(out=lam_raw[:], in_=lam.rearrange("(g p t) -> p g t", g=GROUPS, t=4))
             make_identity(nc, ident[:])
-            for q in range(4):
-                load_scale_rows(e_scale_raw, fwd_scales, q)
-            for q in range(2):
-                load_scale_rows(x_scale, x_scales, q)
             nc.sync.dma_start(out=e_raw[:].bitcast(I32), in_=fwd_words.rearrange("g p b -> p g b").bitcast(I32))
             load_x(0)
-            for q in range(2, 4):
-                load_scale_rows(x_scale, x_scales, q)
+            for q in range(4):
+                load_scale_rows(e_scale_raw, fwd_scales, q)
+            for q in range(4):
+                load_scale_rows(x_scale_first, x_scales[:, :, 0:ROWS], q)
             load_adj(0)
             load_x(1)
+            for q in range(4):
+                load_scale_rows(x_scale_rest, x_scales[:, :, ROWS : FRAMES * ROWS], q)
             load_adj(1)
             load_coil()
             load_x(2)
@@ -237,7 +257,7 @@ def tile_masked_fourier_soft_threshold_h2_kernel(
                     lhsT=e_words[:, g, 2 * col : 2 * (col + P)].bitcast(FP4X4),
                     lhsT_scale=e_scale[:, g, col : col + P],
                     rhs=x_codes[fr][:, g, :].bitcast(FP8X4),
-                    rhs_scale=x_scale[:, g, ROWS * fr : ROWS * (fr + 1)],
+                    rhs_scale=x_scale_first[:, g, :] if fr == 0 else x_scale_rest[:, g, ROWS * (fr - 1) : ROWS * fr],
                     start=(g == 0),
                     stop=(g == GROUPS - 1),
                 )
@@ -253,8 +273,12 @@ def tile_masked_fourier_soft_threshold_h2_kernel(
 
         def h_weave(fr, gf, c0, c1, engine):
             k = 2 * fr + gf
-            dst = h_woven[k % 3][:, c0:c1, :].rearrange("p (c i) t -> p c t i", i=4)
-            src = h_raw[k % 4][:, :, c0:c1].rearrange("p t (c i) -> p c t i", i=4)
+            if engine == "gpsimd":
+                dst = h_woven[k % 3][:, c0:c1, :]
+                src = h_raw[k % 4][:, :, c0:c1].rearrange("p t c -> p c t")
+            else:
+                dst = h_woven[k % 3][:, c0:c1, :].rearrange("p (c i) t -> p c t i", i=4)
+                src = h_raw[k % 4][:, :, c0:c1].rearrange("p t (c i) -> p c t i", i=4)
             move(engine, dst, src)
 
         def h_quant(fr, gf):
@@ -322,10 +346,7 @@ def tile_masked_fourier_soft_threshold_h2_kernel(
             )
 
         def cast(unit, r0, r1, slot, pslot, engine):
-            for rb in range(r0, r1):
-                dst = y_pairs[pslot][:, rb, :].rearrange("r (u p e) -> r u p e", u=2, e=2)
-                src = y_rows[slot][:, rb, :].rearrange("r (p u e) -> r u p e", u=2, e=2)
-                move(engine, dst, src)
+            move(engine, y_pairs[pslot][:, r0:r1, :], y_rows[slot][:, r0:r1, :])
 
         def word_turn(unit, r0, r1, pslot, index):
             bank = take_bank(("word", unit, r0), index)
@@ -333,7 +354,7 @@ def tile_masked_fourier_soft_threshold_h2_kernel(
             for j in range(r1 - r0):
                 for u in range(2):
                     nc.tensor.transpose(
-                        bank[:, P * (2 * j + u) : P * (2 * j + u + 1)], words[:, r0 + j, P * u : P * (u + 1)], ident[:]
+                        bank[:, P * (2 * j + u) : P * (2 * j + u + 1)], words[:, r0 + j, u : 2 * P : 2], ident[:]
                     )
 
         def word_out(unit, r0, r1, pslot, engine):

from contextlib import ExitStack

import concourse.mybir as mybir
from concourse.masks import make_identity

F32 = mybir.dt.float32
BF16 = mybir.dt.bfloat16
I32 = mybir.dt.int32
U32 = mybir.dt.uint32
U8 = mybir.dt.uint8
FP8X4 = mybir.dt.float8_e4m3fn_x4
FP4X4 = mybir.dt.float4_e2m1fn_x4
ALU = mybir.AluOpType
ACT = mybir.ActivationFunctionType

P = 128
FRAMES = 4
ROWS = 512
GROUPS = 2
FLOPS = 2 * 2 * 2048 * 1024 * 1024

HEAD = [('e_perm',), ('mask_perm',), 'm', ('e_scale_perm',), ('mask_out',), ('lam',), ('adj_weave', 0, 0, 0, 2, 'scalar'), ('adj_weave', 0, 0, 2, 4, 'vector'), 's', 's', 's', 's', ('adj_weave', 1, 0, 0, 4, 'vector'), ('adj_quant', 0, 0), ('h_weave', 0, 0, 0, 512, 'vector'), ('adj_quant', 1, 0), 's', 's', 's', 's', ('h_quant', 0, 0), ('h_weave', 0, 1, 0, 192, 'scalar'), ('h_weave', 0, 1, 192, 512, 'vector'), ('h_quant', 0, 1), 's', 's', 's', 's', 's', 's', ('adj_weave', 0, 1, 0, 4, 'vector'), ('adj_weave', 1, 1, 0, 4, 'vector')]
EARLY = {0: [('h_weave', 1, 0, 128, 512, 'gpsimd')], 1: [('h_weave', 1, 1, 256, 384, 'gpsimd'), ('h_weave', 2, 0, 0, 128, 'gpsimd')], 2: [('h_weave', 2, 1, 0, 128, 'gpsimd'), ('h_weave', 2, 1, 384, 512, 'gpsimd')], 3: [('h_weave', 3, 0, 384, 512, 'gpsimd')]}
SIDE = {0: ['s', 's', 's', 's', 's', 's'], 1: ['s', 's', 's', ('h_weave', 1, 1, 128, 256, 'scalar'), 's', 's', ('h_weave', 2, 0, 384, 512, 'scalar')], 2: ['s', 's', 's', ('h_weave', 2, 0, 128, 256, 'scalar'), ('h_weave', 2, 1, 128, 256, 'scalar')], 3: ['s', ('h_weave', 2, 1, 256, 384, 'scalar'), ('h_weave', 3, 0, 128, 256, 'scalar')], 4: ['s', 's', 's', ('h_weave', 3, 0, 256, 384, 'scalar'), ('h_weave', 3, 1, 128, 384, 'scalar')], 5: [('h_weave', 3, 1, 0, 128, 'scalar'), ('h_weave', 3, 1, 384, 512, 'scalar')]}
WINDOW = {0: [('h_weave', 1, 0, 0, 128, 'vector'), ('adj_quant', 0, 1), ('adj_quant', 1, 1), ('h_quant', 1, 0)], 1: [('h_weave', 1, 1, 0, 128, 'vector'), ('h_weave', 1, 1, 384, 512, 'vector'), ('h_weave', 2, 0, 256, 384, 'vector'), ('h_quant', 1, 1)], 3: [('h_weave', 3, 0, 0, 128, 'vector'), ('h_quant', 2, 0), ('h_quant', 2, 1)], 5: [('h_quant', 3, 0), ('h_quant', 3, 1)]}
AHEAD = {3: 1}
WORDS_BEFORE = {1: [0], 3: [1, 2], 5: [3], 6: [4, 5], 7: [6]}
WORDS_AFTER = {}
PLANES = {2: [0], 4: [1, 2], 6: [3, 4], 7: [5], 8: [6]}
LAST_CAST = ("gpsimd", "scalar", "gpsimd", "scalar")
TAIL = ((0, 2), (2, 3), (3, 4))
YS = 3
CW = 1


def schedule():
    units = [(fr, g) for fr in range(FRAMES) for g in range(GROUPS)]
    count = len(units)
    todo = [(fr, gf, t) for fr in range(FRAMES) for gf in range(GROUPS) for t in range(4)]
    taken = []

    def bank():
        taken.append(len(taken) % 8)
        return taken[-1]

    def side(items):
        out = []
        for e in items:
            if e == "s":
                b = todo.pop(0)
                out += [("spec_mm",) + b + (bank(),), ("spec_out",) + b + ("scalar",)]
            elif e == "m":
                out += [("mask_turn", bank())]
            else:
                out += [e]
        return out

    def pix(k, ts):
        if k >= count:
            return []
        return [("pix_mm", units[k], t, bank()) for t in ts] + [("relu", units[k], t) for t in ts] + [("soft", units[k], t, k % 2) for t in ts]

    def words(u, cuts):
        out = []
        for r0, r1 in cuts:
            out += [("word_turn", units[u], r0, r1, u % 2, bank()), ("word_out", units[u], r0, r1, u % 3, "scalar")]
        return out

    def planes(u, cuts):
        out = []
        for r0, r1 in cuts:
            out += [("plane_quant", units[u], P * r0, P * r1, u % 3, u % 3), ("word_store", units[u], P * r0, P * r1, u % 3)]
        return out

    ops = [("setup",)] + side(HEAD)
    for k in range(count + 1):
        if k >= 1:
            for rb in range(4):
                ops += [("y_out", units[k - 1], rb, (k - 1) % YS)]
                if k == count:
                    ops += [("y_store", units[k - 1], rb, rb + 1, (k - 1) % YS)]
                    ops += [("cast", units[k - 1], rb, rb + 1, (k - 1) % YS, (k - 1) % 2, LAST_CAST[rb])]
                elif (rb + 1) % CW == 0:
                    ops += [("cast", units[k - 1], rb + 1 - CW, rb + 1, (k - 1) % YS, (k - 1) % 2, "gpsimd")]
                if k < count and rb % 2 == 1:
                    ops += [("y_store", units[k - 1], rb - 1, rb + 1, (k - 1) % YS)]
        ops += EARLY.get(k, [])
        ops += pix(k, range(AHEAD.get(k, 0), 4)) + pix(k + 1, range(AHEAD.get(k + 1, 0)))
        ops += side(SIDE.get(k, []))
        for u in WORDS_BEFORE.get(k, []):
            ops += words(u, ((0, 2), (2, 4)))
        if k < count:
            ops += [("turn", units[k], rb, k % 2, bank()) for rb in range(4)]
        for u in WORDS_AFTER.get(k, []):
            ops += words(u, ((0, 2), (2, 4)))
        if k == count:
            ops += words(count - 1, TAIL)
        ops += WINDOW.get(k, [])
        for u in PLANES.get(k, []):
            ops += planes(u, ((0, 4),))
            if u == 5:
                ops += [("scale_store", 0, 3 * ROWS)]
    ops += planes(count - 1, TAIL) + [("scale_store", 3 * ROWS, 4 * ROWS)]
    return ops


def tile_masked_fourier_soft_threshold_h2_kernel(
    tc, x_words, x_scales, fwd_words, fwd_scales, mask, adj, lam, coil, out_0, out_1, out_2
):
    nc = tc.nc
    with ExitStack() as ctx:
        sb = ctx.enter_context(tc.tile_pool(name="sb", bufs=1))
        ps = ctx.enter_context(tc.psum_pool(name="ps", bufs=1))
        ctx.enter_context(tc.manual_schedule())

        def tiles(name, count, shape, dtype):
            return [sb.tile(shape, dtype, name="%s%d" % (name, i), align_bytes=64) for i in range(count)]

        banks = [ps.tile([P, 512], F32, name="bank%d" % i) for i in range(8)]
        e_raw = sb.tile([P, GROUPS, 2048], U8, align_bytes=64)
        e_words = sb.tile([P, GROUPS, 2048], U8, align_bytes=64)
        e_scale_raw = sb.tile([P, GROUPS, 1024], U8, align_bytes=64)
        e_scale = sb.tile([P, GROUPS, 1024], U8, align_bytes=64)
        x_codes = tiles("x_codes", FRAMES, [P, GROUPS, ROWS], U32)
        x_scale_first = sb.tile([P, GROUPS, ROWS], U8, align_bytes=64)
        x_scale_rest = sb.tile([P, GROUPS, (FRAMES - 1) * ROWS], U8, align_bytes=64)
        adj_raw = tiles("adj_raw", 4, [P, 4, 512], BF16)
        adj_woven = tiles("adj_woven", 4, [P, 2048], BF16)
        adj_codes = tiles("adj_codes", 4, [P, 512], U32)
        adj_scale = tiles("adj_scale", 4, [P, 512], U8)
        coil_rows = sb.tile([P, 4, 1024], BF16, align_bytes=64)
        ident = sb.tile([P, P], F32, align_bytes=64)
        mask_raw = sb.tile([8, 512], BF16, align_bytes=64)
        mask_rows = sb.tile([P, 512], F32, align_bytes=64)
        mask_cols = sb.tile([P, 4, 8], F32, align_bytes=64)
        lam_raw = sb.tile([P, GROUPS, 4], BF16, align_bytes=64)
        lam_abs = sb.tile([P, GROUPS, 4], F32, align_bytes=64)
        lam_lift = sb.tile([P, GROUPS, 4], F32, align_bytes=64)
        lam_bias = sb.tile([P, GROUPS, 4], F32, align_bytes=64)
        warm = sb.tile([P, 1], F32, align_bytes=64)
        h_raw = tiles("h_raw", 4, [P, 4, ROWS], BF16)
        h_woven = tiles("h_woven", 2, [P, ROWS, 4], BF16) + [adj_raw[3][:].rearrange("p j (a t) -> p (j a) t", t=4)]
        h_codes = tiles("h_codes", 8, [P, ROWS], U32)
        h_scale = tiles("h_scale", 8, [P, ROWS], U8)
        above = tiles("above", 4, [P, ROWS], F32)
        soft = tiles("soft", 2, [P, 4, ROWS], F32)
        y_rows = tiles("y_rows", 3, [P, 4, 512], F32)
        y_pairs = tiles("y_pairs", 2, [P, 4, 512], BF16)
        y_woven = tiles("y_woven", 3, [P, ROWS, 4], BF16)
        y_codes = tiles("y_codes", 3, [P, ROWS], U32)
        y_scale = sb.tile([P, GROUPS, FRAMES * ROWS], U8, align_bytes=64)

        x_hbm = x_words.rearrange("g p n t -> p g (n t)")
        y_hbm = out_0.rearrange("i c l n -> i (c l) n")
        words_hbm = out_1.rearrange("g p m t -> g p (m t)")
        bank_of = {}

        def take_bank(key, index):
            bank_of[key] = banks[index]
            return bank_of[key]

        def move(engine, dst, src):
            if engine == "gpsimd":
                nc.gpsimd.tensor_scalar(out=dst, in0=src, scalar1=1.0, scalar2=1.0, op0=ALU.mult, op1=ALU.mult)
            elif engine == "vector":
                nc.vector.tensor_copy(out=dst, in_=src)
            else:
                nc.scalar.copy(out=dst, in_=src)

        def load_scale_rows(plane, rows, q):
            nc.sync.dma_start(
                out=plane[32 * q : 32 * q + 4, :, :].bitcast(I32),
                in_=rows[:, 4 * q : 4 * q + 4, :].rearrange("g r n -> r g n").bitcast(I32),
            )

        def load_x(fr):
            nc.sync.dma_start(out=x_codes[fr][:].bitcast(I32), in_=x_hbm[:, :, 2048 * fr : 2048 * (fr + 1)].bitcast(I32))

        def load_adj(g):
            for gf in range(GROUPS):
                src = adj[512 * gf : 512 * (gf + 1), 512 * g : 512 * (g + 1)].rearrange("(q t b) n -> b q t n", t=4, b=4)
                for b in range(4):
                    nc.sync.dma_start(out=adj_raw[2 * gf + g][b:P:4, :, :], in_=src[b])

        def load_coil():
            nc.sync.dma_start(out=coil_rows[:], in_=coil.rearrange("c l n -> (c l) n").rearrange("(b r) n -> r b n", r=P))

        def setup():
            nc.vector.memset(e_scale_raw[:].bitcast(I32), 0)
            nc.vector.memset(x_scale_first[:].bitcast(I32), 0)
            nc.vector.memset(mask_rows[:], 0.0)
            nc.vector.memset(x_scale_rest[:].bitcast(I32), 0)
            nc.vector.memset(warm[:], 0.0)
            nc.scalar.activation(out=warm[:], in_=warm[:], func=ACT.Relu)
            nc.gpsimd.dma_start(out=mask_raw[:], in_=mask.rearrange("i (g f) -> (i g) f", g=GROUPS))
            nc.gpsimd.dma_start(out=lam_raw[:], in_=lam.rearrange("(g p t) -> p g t", g=GROUPS, t=4))
            make_identity(nc, ident[:])
            nc.sync.dma_start(out=e_raw[:].bitcast(I32), in_=fwd_words.rearrange("g p b -> p g b").bitcast(I32))
            load_x(0)
            for q in range(4):
                load_scale_rows(e_scale_raw, fwd_scales, q)
            for q in range(4):
                load_scale_rows(x_scale_first, x_scales[:, :, 0:ROWS], q)
            load_adj(0)
            load_x(1)
            for q in range(4):
                load_scale_rows(x_scale_rest, x_scales[:, :, ROWS : FRAMES * ROWS], q)
            load_adj(1)
            load_coil()
            load_x(2)
            load_x(3)

        def e_scale_perm():
            nc.vector.tensor_copy(
                out=e_scale[:].bitcast(I32).rearrange("p g (h t q) -> p (g h) t q", h=2, t=4),
                in_=e_scale_raw[:].bitcast(I32).rearrange("p g (h q t) -> p (g h) t q", h=2, t=4),
            )

        def e_perm():
            for gf in range(GROUPS):
                for g in range(GROUPS):
                    cols = slice(256 * gf, 256 * (gf + 1))
                    nc.vector.tensor_copy(
                        out=e_words[:].bitcast(I32)[:, g, cols].rearrange("p (t q b) -> p t q b", t=4, b=2),
                        in_=e_raw[:].bitcast(I32)[:, g, cols].rearrange("p (q t b) -> p t q b", t=4, b=2),
                    )

        def mask_perm():
            nc.vector.tensor_copy(
                out=mask_rows[0:8, :].rearrange("p (t q b) -> p t q b", t=4, b=4),
                in_=mask_raw[:].rearrange("p (q t b) -> p t q b", t=4, b=4),
            )

        def mask_turn(index):
            bank = take_bank("mask", index)
            for t in range(4):
                nc.tensor.transpose(bank[:, P * t : P * (t + 1)], mask_rows[:, P * t : P * (t + 1)], ident[:])

        def mask_out():
            nc.vector.tensor_copy(out=mask_cols[:], in_=bank_of["mask"][:].rearrange("p (t r) -> p t r", t=4)[:, :, 0:8])

        def lam_prepare():
            nc.vector.scalar_tensor_tensor(
                out=lam_abs[:], in0=lam_raw[:], scalar=-1.0, in1=lam_raw[:], op0=ALU.mult, op1=ALU.max
            )
            nc.gpsimd.tensor_scalar(
                out=lam_lift[:], in0=lam_raw[:], scalar1=0.0, scalar2=2.0**126, op0=ALU.is_lt, op1=ALU.mult
            )
            nc.gpsimd.tensor_tensor(out=lam_bias[:], in0=lam_lift[:], in1=lam_raw[:], op=ALU.subtract)

        def spec_mm(fr, gf, t, index):
            bank = take_bank(("spec", fr, gf, t), index)
            col = 512 * gf + P * t
            for g in range(GROUPS):
                nc.tensor.matmul_mx(
                    out=bank[:],
                    lhsT=e_words[:, g, 2 * col : 2 * (col + P)].bitcast(FP4X4),
                    lhsT_scale=e_scale[:, g, col : col + P],
                    rhs=x_codes[fr][:, g, :].bitcast(FP8X4),
                    rhs_scale=x_scale_first[:, g, :] if fr == 0 else x_scale_rest[:, g, ROWS * (fr - 1) : ROWS * fr],
                    start=(g == 0),
                    stop=(g == GROUPS - 1),
                )

        def spec_out(fr, gf, t, engine):
            k = 2 * fr + gf
            bank = bank_of[("spec", fr, gf, t)]
            factor = mask_cols[:, t, k : k + 1]
            if engine == "vector":
                nc.vector.tensor_scalar(out=h_raw[k % 4][:, t, :], in0=bank[:], scalar1=factor, scalar2=None, op0=ALU.mult)
            else:
                nc.scalar.activation(out=h_raw[k % 4][:, t, :], in_=bank[:], func=ACT.Copy, scale=factor)

        def h_weave(fr, gf, c0, c1, engine):
            k = 2 * fr + gf
            if engine == "gpsimd":
                dst = h_woven[k % 3][:, c0:c1, :]
                src = h_raw[k % 4][:, :, c0:c1].rearrange("p t c -> p c t")
            else:
                dst = h_woven[k % 3][:, c0:c1, :].rearrange("p (c i) t -> p c t i", i=4)
                src = h_raw[k % 4][:, :, c0:c1].rearrange("p t (c i) -> p c t i", i=4)
            move(engine, dst, src)

        def h_quant(fr, gf):
            k = 2 * fr + gf
            nc.vector.quantize_mx(
                out=h_codes[k][:].bitcast(FP8X4), scales=h_scale[k][:],
                in_=h_woven[k % 3][:].rearrange("p r t -> p (r t)"),
            )

        def adj_weave(gf, g, t0, t1, engine):
            dst = adj_woven[2 * gf + g][:].rearrange("p (t m j) -> p t m j", t=4, j=4)[:, t0:t1]
            src = adj_raw[2 * gf + g][:].rearrange("p j (m t) -> p t m j", t=4)[:, t0:t1]
            move(engine, dst, src)

        def adj_quant(gf, g):
            k = 2 * gf + g
            nc.vector.quantize_mx(out=adj_codes[k][:].bitcast(FP8X4), scales=adj_scale[k][:], in_=adj_woven[k][:])

        def pix_mm(unit, t, index):
            fr, g = unit
            bank = take_bank(("pix", unit, t), index)
            for gf in range(GROUPS):
                nc.tensor.matmul_mx(
                    out=bank[:],
                    lhsT=adj_codes[2 * gf + g][:, P * t : P * (t + 1)].bitcast(FP8X4),
                    lhsT_scale=adj_scale[2 * gf + g][:, P * t : P * (t + 1)],
                    rhs=h_codes[2 * fr + gf][:].bitcast(FP8X4),
                    rhs_scale=h_scale[2 * fr + gf][:],
                    start=(gf == 0),
                    stop=(gf == GROUPS - 1),
                )

        def relu(unit, t):
            fr, g = unit
            nc.scalar.activation(
                out=above[t][:], in_=bank_of[("pix", unit, t)][:], func=ACT.Relu, bias=lam_bias[:, g, t : t + 1]
            )

        def soft_min(unit, t, slot):
            fr, g = unit
            nc.vector.scalar_tensor_tensor(
                out=soft[slot][:, t, :], in0=bank_of[("pix", unit, t)][:], scalar=lam_abs[:, g, t : t + 1],
                in1=above[t][:], op0=ALU.add, op1=ALU.min,
            )

        def turn(unit, rb, slot, index):
            bank = take_bank(("turn", unit, rb), index)
            for t in range(4):
                nc.tensor.transpose(bank[:, P * t : P * (t + 1)], soft[slot][:, t, P * rb : P * (rb + 1)], ident[:])

        def y_out(unit, rb, slot):
            fr, g = unit
            nc.vector.tensor_tensor(
                out=y_rows[slot][:, rb, :].rearrange("r (p t) -> r p t", t=4),
                in0=bank_of[("turn", unit, rb)][:].rearrange("r (t p) -> r p t", t=4),
                in1=coil_rows[:, rb, 512 * g : 512 * (g + 1)].rearrange("r (p t) -> r p t", t=4),
                op=ALU.mult,
            )

        def y_store(unit, r0, r1, slot):
            fr, g = unit
            nc.sync.dma_start(
                out=y_hbm[fr].rearrange("(b r) n -> r b n", r=P)[:, r0:r1, 512 * g : 512 * (g + 1)],
                in_=y_rows[slot][:, r0:r1, :],
            )

        def cast(unit, r0, r1, slot, pslot, engine):
            move(engine, y_pairs[pslot][:, r0:r1, :], y_rows[slot][:, r0:r1, :])

        def word_turn(unit, r0, r1, pslot, index):
            bank = take_bank(("word", unit, r0), index)
            words = y_pairs[pslot][:].bitcast(F32)
            for j in range(r1 - r0):
                for u in range(2):
                    nc.tensor.transpose(
                        bank[:, P * (2 * j + u) : P * (2 * j + u + 1)], words[:, r0 + j, u : 2 * P : 2], ident[:]
                    )

        def word_out(unit, r0, r1, pslot, engine):
            dst = y_woven[pslot][:, P * r0 : P * r1, :].rearrange("p r t -> p (r t)").bitcast(F32)
            src = bank_of[("word", unit, r0)][:, 0 : 2 * P * (r1 - r0)]
            move(engine, dst.rearrange("p (j r u) -> p j r u", r=P, u=2), src.rearrange("p (j u r) -> p j r u", r=P, u=2))

        def plane_quant(unit, c0, c1, pslot, slot):
            fr, g = unit
            nc.vector.quantize_mx(
                out=y_codes[slot][:, c0:c1].bitcast(FP8X4),
                scales=y_scale[:, g, ROWS * fr + c0 : ROWS * fr + c1],
                in_=y_woven[pslot][:, c0:c1, :].rearrange("p r t -> p (r t)"),
            )

        def word_store(unit, c0, c1, slot):
            fr, g = unit
            nc.sync.dma_start(
                out=words_hbm[g][:, 4 * (ROWS * fr + c0) : 4 * (ROWS * fr + c1)].bitcast(I32),
                in_=y_codes[slot][:, c0:c1].bitcast(I32),
            )

        def scale_store(c0, c1):
            for q in range(4):
                queue = nc.scalar if (c1 == FRAMES * ROWS and q % 2 == 1) else nc.sync
                queue.dma_start(
                    out=out_2[:, 4 * q : 4 * q + 4, c0:c1].rearrange("g r n -> r g n").bitcast(I32),
                    in_=y_scale[32 * q : 32 * q + 4, :, c0:c1].bitcast(I32),
                )

        steps = {
            "setup": setup, "e_perm": e_perm, "e_scale_perm": e_scale_perm, "mask_perm": mask_perm,
            "mask_turn": mask_turn, "mask_out": mask_out, "lam": lam_prepare, "spec_mm": spec_mm, "spec_out": spec_out,
            "h_weave": h_weave, "h_quant": h_quant, "adj_weave": adj_weave, "adj_quant": adj_quant,
            "cast": cast, "word_turn": word_turn, "word_out": word_out, "pix_mm": pix_mm, "relu": relu, "soft": soft_min,
            "turn": turn, "y_out": y_out, "y_store": y_store, "plane_quant": plane_quant,
            "word_store": word_store, "scale_store": scale_store,
        }
        for step in schedule():
            steps[step[0]](*step[1:])
